import numpy as np
import ml_dtypes


def mxq(x, axis, fmt="e4m3"):
    dtype, down = {"e4m3": (ml_dtypes.float8_e4m3fn, 7), "e5m2": (ml_dtypes.float8_e5m2, 14)}[fmt]
    v = np.moveaxis(np.asarray(x, np.float32).astype(ml_dtypes.bfloat16).astype(np.float64), axis, -1)
    blocks = v.reshape(v.shape[:-1] + (-1, 32))
    amax = np.abs(blocks).max(-1, keepdims=True)
    byte = np.maximum(np.where(amax > 0, np.frexp(amax)[1] - 1 + 127, 0) - down, 1)
    scale = np.exp2(byte - 127.0)
    codes = (blocks / scale).astype(np.float32).astype(dtype).astype(np.float64)
    return np.moveaxis((codes * scale).reshape(v.shape), -1, axis)


WIDE = False


def mx_kscale(k):
    if not WIDE:
        return np.ones(k)
    levels = np.array([10, -10, 5, -5, 0])
    if k % 512:
        return np.exp2(np.random.permutation(np.resize(levels, k // 32))).repeat(32)
    a = np.empty((k // 512, 16))
    for p in range(k // 512):
        a[p, :8] = np.random.permutation(np.resize(levels, 8))
        for g in range(8):
            far = levels[np.abs(levels - a[p, g]) >= 10]
            a[p, g + 8] = far[np.random.randint(len(far))]
    return np.exp2(a.ravel()).repeat(32)


def f64(x):
    return np.asarray(x).astype(np.float64)


def striped(idx):
    return np.tile(idx.reshape(-1, 16).T, (8, 1)).astype(np.uint16)


def unstriped(offs):
    return offs[:16].T.reshape(-1).astype(np.int64)


def pack_weight(w):
    k, n = w.shape
    w = f64(np.asarray(w, np.float32).astype(ml_dtypes.bfloat16)).reshape(k // 32, 32, n)
    amax = np.abs(w).max(1)
    byte = np.clip(np.where(amax > 0, np.frexp(amax)[1] - 1 + 127 - 7, 1), 1, 254)
    scaled = (w * np.exp2(127.0 - byte)[:, None, :]).reshape(k, n).astype(np.float32)
    words = np.ascontiguousarray(scaled.reshape(k // 512, 128, 4, n).transpose(0, 1, 3, 2)).astype(ml_dtypes.float8_e4m3fn).view(np.uint8)
    return words, np.ascontiguousarray(byte.astype(np.uint8).reshape(k // 512, 16, n))


def unpack_weight(words, scales):
    g, p, n, _ = words.shape
    vals = np.ascontiguousarray(words).view(ml_dtypes.float8_e4m3fn).astype(np.float64) * np.repeat(np.exp2(scales.astype(np.float64) - 127.0), 8, axis=1)[..., None]
    return vals.transpose(0, 1, 3, 2).reshape(g * 512, n)


def relu(v):
    return np.maximum(v, 0.0)


K, T, S, N, H, W, U = 512, 1024, 512, 256, 512, 1024, 1024


def setup_inputs():
    n = np.random.standard_normal
    s = mx_kscale(K)[:, None]
    u = mx_kscale(H)
    packed_xT = pack_weight(n((K, T)) * s)
    packed_eT = pack_weight(n((K, W)) * s)
    return {
        "x_words": packed_xT[0],
        "x_scales": packed_xT[1],
        "w1": (n((K, H)) / np.sqrt(K) / s).astype(np.float32),
        "e_words": packed_eT[0],
        "e_scales": packed_eT[1],
        "w2": (n((K, H)) / np.sqrt(K) / s).astype(np.float32),
        "imp": (np.random.uniform(0.3, 1.3, (H, U))).astype(np.float32),
        "unit": (np.random.uniform(0.6, 1.4, (H, 1)) * u[:, None]).astype(np.float32),
        "w3": (n((H, N)) / np.sqrt(H) / u[:, None]).astype(np.float32),
        "offs": striped(np.random.permutation(T)[:S]),
        "rem": striped(np.random.permutation(W)[:S]),
        "qu": striped(np.random.permutation(np.concatenate([np.arange(S), np.random.randint(0, S, U - S)]))),
        "re": striped(np.random.permutation(np.concatenate([np.arange(S), np.random.randint(0, S, U - S)]))),
        "hsh": striped(np.random.permutation(S)),
    }


def reference(x_words, x_scales, w1, e_words, e_scales, w2, imp, unit, w3, offs, rem, qu, re, hsh):
    xq = unpack_weight(x_words, x_scales)[:, unstriped(offs)]
    y = mxq(f64(w1), 0, "e4m3").T @ xq
    gq = y[:, unstriped(qu)]
    e_rem = unpack_weight(e_words, e_scales)[:, unstriped(rem)]
    ye = mxq(f64(w2), 0, "e4m3").T @ e_rem
    gr = ye[:, unstriped(re)]
    emb = gq * gr
    mixd = y[:, unstriped(hsh)] - ye
    emb2 = emb + f64(imp) * mixd[:, unstriped(re)]
    hid = f64(unit) * relu(emb2)
    return mxq(f64(w3), 0, "e4m3").T @ mxq(hid, 0, "e4m3")

@@ -1,0 +1,277 @@
+from contextlib import ExitStack
+
+import concourse.mybir as mybir
+from concourse.masks import make_identity
+
+K, T, S, N, H, U = 512, 1024, 512, 256, 512, 1024
+FLOPS = 2 * (2 * K * H * S + H * N * U)
+
+F32 = mybir.dt.float32
+BF16 = mybir.dt.bfloat16
+I32 = mybir.dt.int32
+U32 = mybir.dt.uint32
+U16 = mybir.dt.uint16
+U8 = mybir.dt.uint8
+FP8X4 = mybir.dt.float8_e4m3fn_x4
+ALU = mybir.AluOpType
+ACT = mybir.ActivationFunctionType
+
+P = 128
+PACK = 4
+TILES = H // P
+HALF = 256
+WINDOW = S + 16
+CHUNKS = (512, 384, 128)
+RING = 4
+
+
+def tile_picked_yqrcmp_relu_p_kernel(
+    tc, x_words, x_scales, w1, e_words, e_scales, w2, imp, unit, w3, offs, rem, qu, re, hsh, out
+):
+    nc = tc.nc
+    with ExitStack() as ctx:
+        lists = ctx.enter_context(tc.tile_pool(name="lists", bufs=1))
+        keep = ctx.enter_context(tc.tile_pool(name="keep", bufs=1))
+        psum = ctx.enter_context(tc.psum_pool(name="psum", bufs=1))
+
+        def load_list(name, src):
+            dst = lists.tile(list(src.shape), U16, name=name)
+            nc.sync.dma_start(dst[:], src)
+            return dst
+
+        def load_words(name, src):
+            dst = keep.tile([P, T], I32, name=name)
+            nc.sync.dma_start(dst[:], src[0].rearrange("p n t -> p (n t)").bitcast(I32))
+            return dst
+
+        def load_scales(dst, src):
+            for q in range(4):
+                nc.sync.dma_start(dst[32 * q : 32 * q + 4, :].bitcast(I32), src[0, 4 * q : 4 * q + 4, :].bitcast(I32))
+
+        def load_weight_half(name, src, half):
+            dst = keep.tile([P, PACK, HALF], F32, name=name)
+            nc.sync.dma_start(dst[:], src.rearrange("(p j) c -> p j c", j=PACK)[:, :, HALF * half : HALF * half + HALF])
+            return dst
+
+        def load_imp(t):
+            dst = keep.tile([P, U], F32, name="imp%d" % t)
+            nc.sync.dma_start(dst[:], imp[P * t : P * t + P, :])
+            return dst
+
+        xs_all = keep.tile([P, T], U8, name="xs_all")
+        es_all = keep.tile([P, T], U8, name="es_all")
+        nc.vector.memset(xs_all[:].bitcast(I32), 0)
+        nc.vector.memset(es_all[:].bitcast(I32), 0)
+
+        offs_t = load_list("offs_t", offs)
+        xw_all = load_words("xw_all", x_words)
+        w1_raw = [load_weight_half("w1_raw0", w1, 0)]
+        load_scales(xs_all, x_scales)
+        rem_t = load_list("rem_t", rem)
+        ew_all = load_words("ew_all", e_words)
+        load_scales(es_all, e_scales)
+        w2_raw = [load_weight_half("w2_raw0", w2, 0)]
+        unit_rows = keep.tile([P, TILES], F32, name="unit_rows")
+        with nc.allow_non_contiguous_dma(reason="one value a partition"):
+            nc.sync.dma_start(unit_rows[:], unit.rearrange("(t p) o -> p (t o)", p=P))
+        qu_t = load_list("qu_t", qu)
+        hsh_t = load_list("hsh_t", hsh)
+        re_t = load_list("re_t", re)
+        w1_raw.append(load_weight_half("w1_raw1", w1, 1))
+        imp_t = [load_imp(0)]
+        w2_raw.append(load_weight_half("w2_raw1", w2, 1))
+        imp_t.append(load_imp(1))
+        unit_k = keep.tile([P, PACK], F32, name="unit_k")
+        nc.sync.dma_start(unit_k[:], unit.rearrange("(p j) o -> p (j o)", j=PACK))
+        w3_raw = load_weight_half("w3_raw", w3, 0)
+        imp_t.append(load_imp(2))
+        imp_t.append(load_imp(3))
+
+        ident = keep.tile([P, P], F32, name="ident")
+        make_identity(nc, ident[:])
+
+        def sign_of(name, src):
+            twice = keep.tile([P, 4], F32, name=name + "_twice")
+            nc.gpsimd.tensor_scalar(twice[:], src[:], 0.0, 2.0, ALU.is_ge, ALU.mult)
+            dst = keep.tile([P, 4], F32, name=name)
+            nc.gpsimd.tensor_scalar(dst[:], twice[:], 1.0, -1.0, ALU.mult, ALU.add)
+            return dst
+
+        sign_rows = sign_of("sign_rows", unit_rows)
+        size = keep.tile([P, TILES], F32, name="size")
+        nc.gpsimd.tensor_tensor(size[:], unit_rows[:], sign_rows[:], ALU.mult)
+        neg_size = keep.tile([P, TILES], F32, name="neg_size")
+        nc.gpsimd.tensor_scalar(neg_size[:], size[:], -1.0, 0.0, ALU.mult, ALU.add)
+        sign_k = sign_of("sign_k", unit_k)
+
+        banks = [psum.tile([P, S], F32, name="bank%d" % i) for i in range(8)]
+
+        def scratch(name):
+            return keep.tile([P, S], F32, name=name, align_bytes=64)
+
+        gq_ring = [scratch("gq%d" % i) for i in range(2)]
+        emb_ring = [scratch("emb%d" % i) for i in range(RING)]
+        hashed_ring = [scratch("hashed%d" % i) for i in range(RING)]
+        staged = [scratch("staged%d" % i) for i in range(6)]
+        hid_rows = [keep.tile([P, n // P, H], BF16, name="hid_rows%d" % i) for i, n in enumerate(CHUNKS)]
+
+        def interleave(dst, src):
+            nc.scalar.copy(
+                dst.rearrange("p (c i j) -> p c j i", i=4, j=PACK), src.rearrange("p j (c i) -> p c j i", i=4)
+            )
+
+        def quantize(name, grouped, width):
+            codes = keep.tile([P, width], U32, name=name + "_codes", align_bytes=64)
+            scales = keep.tile([P, width], U8, name=name + "_scales", align_bytes=64)
+            nc.vector.quantize_mx(out=codes[:].bitcast(FP8X4), scales=scales[:], in_=grouped)
+            return codes, scales
+
+        def weight_operand(name, raw, stage):
+            grouped = stage[:].bitcast(BF16)
+            interleave(grouped, raw)
+            return quantize(name, grouped, HALF)
+
+        def product(acc, weight, c0, words, word_scales):
+            nc.tensor.matmul_mx(
+                out=acc, lhsT=weight[0][:, c0 : c0 + P].bitcast(FP8X4), lhsT_scale=weight[1][:, c0 : c0 + P],
+                rhs=words.bitcast(FP8X4), rhs_scale=word_scales, start=True, stop=True,
+            )
+
+        y_win = [keep.tile([P, WINDOW], F32, name="y%d" % t) for t in range(TILES)]
+        ye_win = [keep.tile([P, WINDOW], F32, name="ye%d" % t) for t in range(TILES)]
+        mix_win = [keep.tile([P, WINDOW], F32, name="mix%d" % t) for t in range(TILES)]
+        neg_ye = [keep.tile([P, S], F32, name="neg_ye%d" % t) for t in range(TILES)]
+
+        xw = keep.tile([P, S], U32, name="xw", align_bytes=64)
+        xs = keep.tile([P, S], U8, name="xs", align_bytes=64)
+        es = keep.tile([P, S], U8, name="es", align_bytes=64)
+        nc.vector.tensor_copy(xw[:], xw_all[:].bitcast(U32).indirect(offs_t[:]))
+        nc.vector.tensor_copy(xs[:], xs_all[:].indirect(offs_t[:]))
+        first_stage = keep.tile([P, S], F32, name="first_stage", tag="shared", align_bytes=64)
+        w1_q = weight_operand("w1a", w1_raw[0][:], first_stage)
+        ew = keep.tile([P, S], U32, name="ew", tag="shared", align_bytes=64)
+        nc.vector.tensor_copy(ew[:], ew_all[:].bitcast(U32).indirect(rem_t[:]))
+        nc.vector.tensor_copy(es[:], es_all[:].indirect(rem_t[:]))
+        w2_q = weight_operand("w2a", w2_raw[0][:], staged[5])
+
+        def y_window(t, weight):
+            acc = banks[t % 2]
+            product(acc[:], weight, P * (t % 2), xw[:], xs[:])
+            nc.scalar.activation(y_win[t][:, :S], acc[:], ACT.Copy, scale=size[:, t : t + 1])
+
+        def ye_windows(t, weight):
+            acc = banks[2 + t % 2]
+            product(acc[:], weight, P * (t % 2), ew[:], es[:])
+            nc.scalar.activation(neg_ye[t][:], acc[:], ACT.Copy, scale=neg_size[:, t : t + 1])
+            nc.scalar.copy(ye_win[t][:, :S], acc[:])
+
+        y_window(0, w1_q)
+        y_window(1, w1_q)
+        ye_windows(0, w2_q)
+        ye_windows(1, w2_q)
+        w1_q = weight_operand("w1b", w1_raw[1][:], emb_ring[1])
+        w2_q = weight_operand("w2b", w2_raw[1][:], hashed_ring[1])
+        for t in (2, 3):
+            y_window(t, w1_q)
+            ye_windows(t, w2_q)
+
+        signed = hid_rows[0][:, :, HALF:]
+        for j in range(PACK):
+            nc.scalar.activation(signed[:, j, :], w3_raw[:, j, :], ACT.Copy, scale=sign_k[:, j : j + 1])
+        w3_q = weight_operand("w3", signed, staged[0])
+
+        starts = [sum(CHUNKS[:i]) for i in range(len(CHUNKS))]
+        gq_of = {4: staged[0], 6: staged[1], 7: staged[2]}
+        turned_bank = [3, 2, 1, 0, 4, 5, 0, 1, 4, 5, 4, 5]
+
+        def gather_gq(step):
+            ci, t = divmod(step, TILES)
+            r0, n = starts[ci], CHUNKS[ci]
+            gq = gq_of.get(step, gq_ring[step % 2])
+            nc.vector.tensor_copy(gq[:, :n], y_win[t][:].indirect(qu_t[:, r0 // 16 : (r0 + n) // 16]))
+
+        def gather_mix(t):
+            nc.vector.tensor_tensor(mix_win[t][:, :S], y_win[t][:].indirect(hsh_t[:]), neg_ye[t][:], ALU.add)
+
+        def gather_emb(step):
+            ci, t = divmod(step, TILES)
+            r0, n = starts[ci], CHUNKS[ci]
+            gq = gq_of.get(step, gq_ring[step % 2])
+            nc.vector.tensor_tensor(
+                emb_ring[step % RING][:, :n], ye_win[t][:].indirect(re_t[:, r0 // 16 : (r0 + n) // 16]), gq[:, :n], ALU.mult
+            )
+
+        def gather_hashed(step):
+            ci, t = divmod(step, TILES)
+            r0, n = starts[ci], CHUNKS[ci]
+            nc.vector.tensor_tensor(
+                hashed_ring[step % RING][:, :n], mix_win[t][:].indirect(re_t[:, r0 // 16 : (r0 + n) // 16]),
+                imp_t[t][:, r0 : r0 + n], ALU.mult,
+            )
+
+        def turn(step, first, second):
+            ci, t = divmod(step, TILES)
+            n = CHUNKS[ci]
+            turned = banks[turned_bank[step]]
+            for b in range(n // P):
+                cols = slice(P * b, P * b + P)
+                nc.tensor.matmul(turned[:, cols], lhsT=first[step % RING][:, cols], rhs=ident[:], start=True, stop=False, is_transpose=True)
+                nc.tensor.matmul(turned[:, cols], lhsT=second[step % RING][:, cols], rhs=ident[:], start=False, stop=True, is_transpose=True)
+            nc.scalar.activation(
+                hid_rows[ci][:, :, P * t : P * t + P], turned[:, :n].rearrange("r (b p) -> r b p", p=P), ACT.Relu
+            )
+
+        def turn_back(ci, b0, blocks, bank, stage):
+            back = bank[:].rearrange("p (b u r) -> p b u r", u=2, r=P)
+            for b in range(blocks):
+                words = hid_rows[ci][:, b0 + b, :].bitcast(F32)
+                for u in range(2):
+                    nc.tensor.transpose(back[:, b, u, :], words[:, u : HALF : 2], ident[:])
+            grouped = stage[:, : 2 * P * blocks]
+            nc.scalar.copy(
+                grouped.rearrange("p (b r u) -> p b r u", r=P, u=2), back[:, :blocks].rearrange("p b u r -> p b r u")
+            )
+            return quantize("hid%d_%d" % (ci, b0), grouped.bitcast(BF16), P * blocks)
+
+        def finish(hid_q, c0, n, bank, on_vector):
+            for m in range(2):
+                product(bank[:, n * m : n * m + n], w3_q, P * m, hid_q[0][:], hid_q[1][:])
+            res = keep.tile([P, 2 * n], F32, name="res%d" % c0)
+            if on_vector:
+                nc.vector.tensor_copy(res[:], bank[:, : 2 * n])
+            else:
+                nc.scalar.copy(res[:], bank[:, : 2 * n])
+            nc.sync.dma_start(
+                out.rearrange("(m p) r -> p m r", p=P)[:, :, c0 : c0 + n], res[:].rearrange("p (m r) -> p m r", m=2)
+            )
+
+        gather_gq(0)
+        gather_gq(1)
+        for t in range(TILES):
+            if t >= 2:
+                gather_gq(t)
+            gather_mix(t)
+            gather_emb(t)
+            gather_hashed(t)
+            turn(t, emb_ring, hashed_ring)
+
+        def step_of(step):
+            gather_gq(step)
+            gather_hashed(step)
+            gather_emb(step)
+            turn(step, hashed_ring, emb_ring)
+
+        q0 = turn_back(0, 0, 2, banks[4], staged[1])
+        q1 = turn_back(0, 2, 2, banks[5], staged[2])
+        finish(q0, 0, 256, banks[6], False)
+        finish(q1, 256, 256, banks[7], False)
+        for step in range(4, 8):
+            step_of(step)
+        q2 = turn_back(1, 0, 2, banks[4], staged[3])
+        q3 = turn_back(1, 2, 1, banks[5], staged[4])
+        for step in range(8, 12):
+            step_of(step)
+        q4 = turn_back(2, 0, 1, banks[2], staged[5])
+        finish(q2, 512, 256, banks[5], False)
+        finish(q3, 768, 128, banks[6], False)
+        finish(q4, 896, 128, banks[7], True)

@@ -19,10 +19,8 @@ ACT = mybir.ActivationFunctionType
 P = 128
 PACK = 4
 TILES = H // P
-HALF = 256
-WINDOW = S + 16
-CHUNKS = (512, 384, 128)
-RING = 4
+A_END, B_END = 512, 896
+WINDOW = B_END + 16
 
 
 def tile_picked_yqrcmp_relu_p_kernel(
@@ -44,13 +42,14 @@ def tile_picked_yqrcmp_relu_p_kernel(
             nc.sync.dma_start(dst[:], src[0].rearrange("p n t -> p (n t)").bitcast(I32))
             return dst
 
-        def load_scales(dst, src):
-            for q in range(4):
-                nc.sync.dma_start(dst[32 * q : 32 * q + 4, :].bitcast(I32), src[0, 4 * q : 4 * q + 4, :].bitcast(I32))
+        def load_scales(dst, src, queue):
+            rows = src[0].bitcast(I32).rearrange("(q r) c -> r q c", r=4)
+            for r in range(4):
+                queue.dma_start(dst[r:P:4, :].bitcast(I32), rows[r].unsqueeze(1).to_broadcast([4, 8, T // 4]))
 
-        def load_weight_half(name, src, half):
-            dst = keep.tile([P, PACK, HALF], F32, name=name)
-            nc.sync.dma_start(dst[:], src.rearrange("(p j) c -> p j c", j=PACK)[:, :, HALF * half : HALF * half + HALF])
+        def load_weight(name, src, c0, c1):
+            dst = keep.tile([P, PACK, c1 - c0], F32, name=name)
+            nc.sync.dma_start(dst[:], src.rearrange("(p j) c -> p j c", j=PACK)[:, :, c0:c1])
             return dst
 
         def load_imp(t):
@@ -60,35 +59,31 @@ def tile_picked_yqrcmp_relu_p_kernel(
 
         xs_all = keep.tile([P, T], U8, name="xs_all")
         es_all = keep.tile([P, T], U8, name="es_all")
-        nc.vector.memset(xs_all[:].bitcast(I32), 0)
-        nc.vector.memset(es_all[:].bitcast(I32), 0)
-
-        offs_t = load_list("offs_t", offs)
-        xw_all = load_words("xw_all", x_words)
-        w1_raw = [load_weight_half("w1_raw0", w1, 0)]
-        load_scales(xs_all, x_scales)
-        rem_t = load_list("rem_t", rem)
-        ew_all = load_words("ew_all", e_words)
-        load_scales(es_all, e_scales)
-        w2_raw = [load_weight_half("w2_raw0", w2, 0)]
         unit_rows = keep.tile([P, TILES], F32, name="unit_rows")
-        with nc.allow_non_contiguous_dma(reason="one value a partition"):
-            nc.sync.dma_start(unit_rows[:], unit.rearrange("(t p) o -> p (t o)", p=P))
+        unit_k = keep.tile([P, PACK], F32, name="unit_k")
+
+        def load_unit_rows():
+            with nc.allow_non_contiguous_dma(reason="one value a partition"):
+                nc.gpsimd.dma_start(unit_rows[:], unit.rearrange("(t p) o -> p (t o)", p=P))
+
+        load_unit_rows()
+        nc.gpsimd.dma_start(unit_k[:], unit.rearrange("(p j) o -> p (j o)", j=PACK))
+        offs_t = load_list("offs_t", offs)
+        load_scales(xs_all, x_scales, nc.sync)
+        xw_all = load_words("xw_all", x_words)
+        w1_first = load_weight("w1_first", w1, 0, P)
+        rem_t = load_list("rem_t", rem)
+        load_scales(es_all, e_scales, nc.sync)
+        ew_all = load_words("ew_all", e_words)
+        w2_first = load_weight("w2_first", w2, 0, P)
         qu_t = load_list("qu_t", qu)
         hsh_t = load_list("hsh_t", hsh)
         re_t = load_list("re_t", re)
-        w1_raw.append(load_weight_half("w1_raw1", w1, 1))
-        imp_t = [load_imp(0)]
-        w2_raw.append(load_weight_half("w2_raw1", w2, 1))
-        imp_t.append(load_imp(1))
-        unit_k = keep.tile([P, PACK], F32, name="unit_k")
-        nc.sync.dma_start(unit_k[:], unit.rearrange("(p j) o -> p (j o)", j=PACK))
-        w3_raw = load_weight_half("w3_raw", w3, 0)
-        imp_t.append(load_imp(2))
-        imp_t.append(load_imp(3))
-
-        ident = keep.tile([P, P], F32, name="ident")
-        make_identity(nc, ident[:])
+        w1_rest = load_weight("w1_rest", w1, P, H)
+        w2_rest = load_weight("w2_rest", w2, P, H)
+        imp_t = [load_imp(0), load_imp(1)]
+        w3_raw = load_weight("w3_raw", w3, 0, N)
+        imp_t.extend([load_imp(2), load_imp(3)])
 
         def sign_of(name, src):
             twice = keep.tile([P, 4], F32, name=name + "_twice")
@@ -102,18 +97,18 @@ def tile_picked_yqrcmp_relu_p_kernel(
         nc.gpsimd.tensor_tensor(size[:], unit_rows[:], sign_rows[:], ALU.mult)
         neg_size = keep.tile([P, TILES], F32, name="neg_size")
         nc.gpsimd.tensor_scalar(neg_size[:], size[:], -1.0, 0.0, ALU.mult, ALU.add)
+        ident = keep.tile([P, P], F32, name="ident")
+        make_identity(nc, ident[:])
         sign_k = sign_of("sign_k", unit_k)
 
         banks = [psum.tile([P, S], F32, name="bank%d" % i) for i in range(8)]
 
-        def scratch(name):
-            return keep.tile([P, S], F32, name=name, align_bytes=64)
+        def scratch(name, width):
+            return keep.tile([P, width], F32, name=name, align_bytes=64)
 
-        gq_ring = [scratch("gq%d" % i) for i in range(2)]
-        emb_ring = [scratch("emb%d" % i) for i in range(RING)]
-        hashed_ring = [scratch("hashed%d" % i) for i in range(RING)]
-        staged = [scratch("staged%d" % i) for i in range(6)]
-        hid_rows = [keep.tile([P, n // P, H], BF16, name="hid_rows%d" % i) for i, n in enumerate(CHUNKS)]
+        hid_a = keep.tile([P, 4, H], BF16, name="hid_a")
+        hid_b = keep.tile([P, 3, H], BF16, name="hid_b")
+        hid_c = keep.tile([P, 1, H], BF16, name="hid_c")
 
         def interleave(dst, src):
             nc.scalar.copy(
@@ -126,10 +121,14 @@ def tile_picked_yqrcmp_relu_p_kernel(
             nc.vector.quantize_mx(out=codes[:].bitcast(FP8X4), scales=scales[:], in_=grouped)
             return codes, scales
 
-        def weight_operand(name, raw, stage):
-            grouped = stage[:].bitcast(BF16)
-            interleave(grouped, raw)
-            return quantize(name, grouped, HALF)
+        def weight_operand(name, parts, stage):
+            c0 = 0
+            grouped = stage.bitcast(BF16)
+            for raw in parts:
+                width = raw.shape[2]
+                interleave(grouped[:, PACK * c0 : PACK * (c0 + width)], raw)
+                c0 += width
+            return quantize(name, grouped[:, : PACK * c0], c0)
 
         def product(acc, weight, c0, words, word_scales):
             nc.tensor.matmul_mx(
@@ -145,133 +144,163 @@ def tile_picked_yqrcmp_relu_p_kernel(
         xw = keep.tile([P, S], U32, name="xw", align_bytes=64)
         xs = keep.tile([P, S], U8, name="xs", align_bytes=64)
         es = keep.tile([P, S], U8, name="es", align_bytes=64)
-        nc.vector.tensor_copy(xw[:], xw_all[:].bitcast(U32).indirect(offs_t[:]))
         nc.vector.tensor_copy(xs[:], xs_all[:].indirect(offs_t[:]))
-        first_stage = keep.tile([P, S], F32, name="first_stage", tag="shared", align_bytes=64)
-        w1_q = weight_operand("w1a", w1_raw[0][:], first_stage)
+        nc.vector.tensor_copy(xw[:], xw_all[:].bitcast(U32).indirect(offs_t[:]))
+        nc.vector.tensor_copy(es[:], es_all[:].indirect(rem_t[:]))
+        w1_stage = keep.tile([P, S], F32, name="w1_stage", tag="shared", align_bytes=64)
+        w1_q = weight_operand("w1", [w1_first[:]], w1_stage[:])
         ew = keep.tile([P, S], U32, name="ew", tag="shared", align_bytes=64)
         nc.vector.tensor_copy(ew[:], ew_all[:].bitcast(U32).indirect(rem_t[:]))
-        nc.vector.tensor_copy(es[:], es_all[:].indirect(rem_t[:]))
-        w2_q = weight_operand("w2a", w2_raw[0][:], staged[5])
+        w2_stage = scratch("w2_stage", 256)
+        w2_q = weight_operand("w2", [w2_first[:]], w2_stage[:])
 
-        def y_window(t, weight):
+        def y_window(t, weight, c0):
             acc = banks[t % 2]
-            product(acc[:], weight, P * (t % 2), xw[:], xs[:])
+            product(acc[:], weight, c0, xw[:], xs[:])
             nc.scalar.activation(y_win[t][:, :S], acc[:], ACT.Copy, scale=size[:, t : t + 1])
 
-        def ye_windows(t, weight):
+        def ye_windows(t, weight, c0):
             acc = banks[2 + t % 2]
-            product(acc[:], weight, P * (t % 2), ew[:], es[:])
+            product(acc[:], weight, c0, ew[:], es[:])
             nc.scalar.activation(neg_ye[t][:], acc[:], ACT.Copy, scale=neg_size[:, t : t + 1])
             nc.scalar.copy(ye_win[t][:, :S], acc[:])
 
-        y_window(0, w1_q)
-        y_window(1, w1_q)
-        ye_windows(0, w2_q)
-        ye_windows(1, w2_q)
-        w1_q = weight_operand("w1b", w1_raw[1][:], emb_ring[1])
-        w2_q = weight_operand("w2b", w2_raw[1][:], hashed_ring[1])
-        for t in (2, 3):
-            y_window(t, w1_q)
-            ye_windows(t, w2_q)
+        gq_ring = [scratch("gq%d" % i, 1024) for i in range(2)]
+        emb_ring = [scratch("emb%d" % i, 1024) for i in range(4)]
+        hashed_ring = [scratch("hashed%d" % i, 1024) for i in range(4)]
 
-        signed = hid_rows[0][:, :, HALF:]
+        y_window(0, w1_q, 0)
+        ye_windows(0, w2_q, 0)
+        second = weight_operand("second", [w1_rest[:, :, :P], w2_rest[:, :, :P]], hashed_ring[0][:])
+        last = weight_operand("last", [w1_rest[:, :, P:], w2_rest[:, :, P:]], gq_ring[1][:])
+        y_window(1, second, 0)
+        ye_windows(1, second, P)
+        for t in (2, 3):
+            y_window(t, last, P * (t - 2))
+            ye_windows(t, last, P * t)
+
+        signed = hid_a[:, :, N:]
         for j in range(PACK):
             nc.scalar.activation(signed[:, j, :], w3_raw[:, j, :], ACT.Copy, scale=sign_k[:, j : j + 1])
-        w3_q = weight_operand("w3", signed, staged[0])
+        w3_stage = scratch("w3_stage", S)
+        w3_q = weight_operand("w3", [signed], w3_stage[:])
 
-        starts = [sum(CHUNKS[:i]) for i in range(len(CHUNKS))]
-        gq_of = {4: staged[0], 6: staged[1], 7: staged[2]}
-        turned_bank = [3, 2, 1, 0, 4, 5, 0, 1, 4, 5, 4, 5]
+        steps = [(0, 0, B_END), (1, 0, B_END), (2, 0, A_END), (3, 0, A_END), (2, A_END, B_END), (3, A_END, B_END)]
+        steps.extend((t, B_END, U) for t in range(TILES))
+
+        stage_a = scratch("stage_a", 1024)
+        gq_to = [gq_ring[i % 2][:] for i in range(10)]
+        emb_to = [emb_ring[i % 4][:] for i in range(10)]
+        hashed_to = [hashed_ring[i % 4][:] for i in range(10)]
+        emb_to[5] = stage_a[:, :384]
+        gq_to[6] = stage_a[:, 384:512]
+        gq_to[8] = stage_a[:, 384:512]
+        for i in range(4):
+            hashed_to[6 + i] = stage_a[:, 512 + P * i : 640 + P * i]
 
         def gather_gq(step):
-            ci, t = divmod(step, TILES)
-            r0, n = starts[ci], CHUNKS[ci]
-            gq = gq_of.get(step, gq_ring[step % 2])
-            nc.vector.tensor_copy(gq[:, :n], y_win[t][:].indirect(qu_t[:, r0 // 16 : (r0 + n) // 16]))
+            t, r0, r1 = steps[step]
+            nc.vector.tensor_copy(gq_to[step][:, : r1 - r0], y_win[t][:].indirect(qu_t[:, r0 // 16 : r1 // 16]))
 
         def gather_mix(t):
             nc.vector.tensor_tensor(mix_win[t][:, :S], y_win[t][:].indirect(hsh_t[:]), neg_ye[t][:], ALU.add)
 
         def gather_emb(step):
-            ci, t = divmod(step, TILES)
-            r0, n = starts[ci], CHUNKS[ci]
-            gq = gq_of.get(step, gq_ring[step % 2])
+            t, r0, r1 = steps[step]
             nc.vector.tensor_tensor(
-                emb_ring[step % RING][:, :n], ye_win[t][:].indirect(re_t[:, r0 // 16 : (r0 + n) // 16]), gq[:, :n], ALU.mult
+                emb_to[step][:, : r1 - r0], ye_win[t][:].indirect(re_t[:, r0 // 16 : r1 // 16]),
+                gq_to[step][:, : r1 - r0], ALU.mult,
             )
 
         def gather_hashed(step):
-            ci, t = divmod(step, TILES)
-            r0, n = starts[ci], CHUNKS[ci]
+            t, r0, r1 = steps[step]
             nc.vector.tensor_tensor(
-                hashed_ring[step % RING][:, :n], mix_win[t][:].indirect(re_t[:, r0 // 16 : (r0 + n) // 16]),
-                imp_t[t][:, r0 : r0 + n], ALU.mult,
+                hashed_to[step][:, : r1 - r0], mix_win[t][:].indirect(re_t[:, r0 // 16 : r1 // 16]),
+                imp_t[t][:, r0:r1], ALU.mult,
             )
 
-        def turn(step, first, second):
-            ci, t = divmod(step, TILES)
-            n = CHUNKS[ci]
-            turned = banks[turned_bank[step]]
-            for b in range(n // P):
-                cols = slice(P * b, P * b + P)
-                nc.tensor.matmul(turned[:, cols], lhsT=first[step % RING][:, cols], rhs=ident[:], start=True, stop=False, is_transpose=True)
-                nc.tensor.matmul(turned[:, cols], lhsT=second[step % RING][:, cols], rhs=ident[:], start=False, stop=True, is_transpose=True)
+        def turn(step, first, then, c0, blocks, dst):
+            for b in range(blocks):
+                cols = slice(c0 + P * b, c0 + P * b + P)
+                to = dst[:, P * b : P * b + P]
+                nc.tensor.matmul(to, lhsT=first[step][:, cols], rhs=ident[:], start=True, stop=False, is_transpose=True)
+                nc.tensor.matmul(to, lhsT=then[step][:, cols], rhs=ident[:], start=False, stop=True, is_transpose=True)
+
+        def relu(hid, t, blocks, bank):
             nc.scalar.activation(
-                hid_rows[ci][:, :, P * t : P * t + P], turned[:, :n].rearrange("r (b p) -> r b p", p=P), ACT.Relu
+                hid[:, :, P * t : P * t + P], bank[:, : P * blocks].rearrange("r (b p) -> r b p", p=P), ACT.Relu
             )
 
-        def turn_back(ci, b0, blocks, bank, stage):
+        def turn_back(hid, b0, blocks, bank, grouped):
             back = bank[:].rearrange("p (b u r) -> p b u r", u=2, r=P)
             for b in range(blocks):
-                words = hid_rows[ci][:, b0 + b, :].bitcast(F32)
+                words = hid[:, b0 + b, :].bitcast(F32)
                 for u in range(2):
-                    nc.tensor.transpose(back[:, b, u, :], words[:, u : HALF : 2], ident[:])
-            grouped = stage[:, : 2 * P * blocks]
+                    nc.tensor.transpose(back[:, b, u, :], words[:, u : 2 * P : 2], ident[:])
             nc.scalar.copy(
                 grouped.rearrange("p (b r u) -> p b r u", r=P, u=2), back[:, :blocks].rearrange("p b u r -> p b r u")
             )
-            return quantize("hid%d_%d" % (ci, b0), grouped.bitcast(BF16), P * blocks)
 
-        def finish(hid_q, c0, n, bank, on_vector):
-            for m in range(2):
-                product(bank[:, n * m : n * m + n], w3_q, P * m, hid_q[0][:], hid_q[1][:])
-            res = keep.tile([P, 2 * n], F32, name="res%d" % c0)
-            if on_vector:
-                nc.vector.tensor_copy(res[:], bank[:, : 2 * n])
-            else:
-                nc.scalar.copy(res[:], bank[:, : 2 * n])
-            nc.sync.dma_start(
-                out.rearrange("(m p) r -> p m r", p=P)[:, :, c0 : c0 + n], res[:].rearrange("p (m r) -> p m r", m=2)
-            )
+        out_rows = out.rearrange("(m p) r -> p m r", p=P)
 
-        gather_gq(0)
-        gather_gq(1)
-        for t in range(TILES):
-            if t >= 2:
-                gather_gq(t)
+        def first_pass(step, bank_a, bank_b):
+            t = steps[step][0]
+            gather_gq(step)
             gather_mix(t)
-            gather_emb(t)
-            gather_hashed(t)
-            turn(t, emb_ring, hashed_ring)
+            gather_emb(step)
+            gather_hashed(step)
+            turn(step, emb_to, hashed_to, 0, 4, bank_a)
+            relu(hid_a, t, 4, bank_a)
+            if steps[step][2] == B_END:
+                turn(step, emb_to, hashed_to, A_END, 3, bank_b)
+                relu(hid_b, t, 3, bank_b)
 
-        def step_of(step):
+        def gathers(step):
             gather_gq(step)
             gather_hashed(step)
             gather_emb(step)
-            turn(step, hashed_ring, emb_ring)
 
-        q0 = turn_back(0, 0, 2, banks[4], staged[1])
-        q1 = turn_back(0, 2, 2, banks[5], staged[2])
-        finish(q0, 0, 256, banks[6], False)
-        finish(q1, 256, 256, banks[7], False)
-        for step in range(4, 8):
-            step_of(step)
-        q2 = turn_back(1, 0, 2, banks[4], staged[3])
-        q3 = turn_back(1, 2, 1, banks[5], staged[4])
-        for step in range(8, 12):
-            step_of(step)
-        q4 = turn_back(2, 0, 1, banks[2], staged[5])
-        finish(q2, 512, 256, banks[5], False)
-        finish(q3, 768, 128, banks[6], False)
-        finish(q4, 896, 128, banks[7], True)
+        first_pass(0, banks[3], banks[2])
+        first_pass(1, banks[3], banks[2])
+        first_pass(2, banks[3], None)
+        first_pass(3, banks[3], None)
+
+        turn_back(hid_a, 0, 2, banks[4], stage_a[:, :512])
+        turn_back(hid_a, 2, 2, banks[5], stage_a[:, 512:])
+        q_a = quantize("hid_a", stage_a[:].bitcast(BF16), A_END)
+        res_a = keep.tile([P, 2, A_END], F32, name="res_a")
+        for m in range(2):
+            product(banks[6 + m][:], w3_q, P * m, q_a[0][:], q_a[1][:])
+            nc.scalar.copy(res_a[:, m, :], banks[6 + m][:])
+        nc.sync.dma_start(out_rows[:, :, :A_END], res_a[:])
+
+        for step in (4, 5):
+            gathers(step)
+            turn(step, hashed_to, emb_to, 0, 3, banks[step])
+            relu(hid_b, steps[step][0], 3, banks[step])
+
+        stage_b = [scratch("stage_b0", 512), scratch("stage_b1", 256)]
+        turn_back(hid_b, 0, 2, banks[1], stage_b[0][:])
+        turn_back(hid_b, 2, 1, banks[0], stage_b[1][:])
+        for step in (6, 7, 8):
+            gathers(step)
+            turn(step, hashed_to, emb_to, 0, 1, banks[1][:, P * (step - 6) :])
+        nc.scalar.activation(hid_c[:, 0, : 3 * P], banks[1][:, : 3 * P], ACT.Relu)
+        gathers(9)
+        turn(9, hashed_to, emb_to, 0, 1, banks[0])
+        relu(hid_c, 3, 1, banks[0])
+        q_b = [quantize("hid_b0", stage_b[0][:].bitcast(BF16), 256), quantize("hid_b1", stage_b[1][:].bitcast(BF16), P)]
+        stage_c = scratch("stage_c", 256)
+        turn_back(hid_c, 0, 1, banks[4], stage_c[:])
+
+        def finish(hid_q, c0, n, bank, copy):
+            for m in range(2):
+                product(bank[:, n * m : n * m + n], w3_q, P * m, hid_q[0][:], hid_q[1][:])
+            res = keep.tile([P, 2 * n], F32, name="res%d" % c0)
+            copy(res[:], bank[:, : 2 * n])
+            nc.sync.dma_start(out_rows[:, :, c0 : c0 + n], res[:].rearrange("p (m r) -> p m r", m=2))
+
+        finish(q_b[0], A_END, 256, banks[1], nc.vector.tensor_copy)
+        q_c = quantize("hid_c", stage_c[:].bitcast(BF16), P)
+        finish(q_b[1], A_END + 256, P, banks[4], nc.scalar.copy)
+        finish(q_c, B_END, P, banks[6], nc.vector.tensor_copy)

@@ -43,9 +43,12 @@ def tile_picked_yqrcmp_relu_p_kernel(
             return dst
 
         def load_scales(dst, src, queue):
-            rows = src[0].bitcast(I32).rearrange("(q r) c -> r q c", r=4)
-            for r in range(4):
-                queue.dma_start(dst[r:P:4, :].bitcast(I32), rows[r].unsqueeze(1).to_broadcast([4, 8, T // 4]))
+            rows = src[0].bitcast(I32)
+            for q in range(4):
+                queue.dma_start(
+                    dst[32 * q : 32 * q + 32, :].bitcast(I32),
+                    rows[4 * q : 4 * q + 4, :].unsqueeze(0).to_broadcast([8, 4, T // 4]),
+                )
 
         def load_weight(name, src, c0, c1):
             dst = keep.tile([P, PACK, c1 - c0], F32, name=name)
@@ -59,15 +62,12 @@ def tile_picked_yqrcmp_relu_p_kernel(
 
         xs_all = keep.tile([P, T], U8, name="xs_all")
         es_all = keep.tile([P, T], U8, name="es_all")
-        unit_rows = keep.tile([P, TILES], F32, name="unit_rows")
+        unit_rows = keep.tile([P, P], F32, name="unit_rows")
         unit_k = keep.tile([P, PACK], F32, name="unit_k")
 
         def load_unit_rows():
-            with nc.allow_non_contiguous_dma(reason="one value a partition"):
-                nc.gpsimd.dma_start(unit_rows[:], unit.rearrange("(t p) o -> p (t o)", p=P))
+            nc.sync.dma_start(unit_rows[:], unit.rearrange("(t p) o -> t (p o)", p=P).unsqueeze(0).to_broadcast([P // TILES, TILES, P]))
 
-        load_unit_rows()
-        nc.gpsimd.dma_start(unit_k[:], unit.rearrange("(p j) o -> p (j o)", j=PACK))
         offs_t = load_list("offs_t", offs)
         load_scales(xs_all, x_scales, nc.sync)
         xw_all = load_words("xw_all", x_words)
@@ -76,14 +76,18 @@ def tile_picked_yqrcmp_relu_p_kernel(
         load_scales(es_all, e_scales, nc.sync)
         ew_all = load_words("ew_all", e_words)
         w2_first = load_weight("w2_first", w2, 0, P)
+        load_unit_rows()
         qu_t = load_list("qu_t", qu)
         hsh_t = load_list("hsh_t", hsh)
         re_t = load_list("re_t", re)
-        w1_rest = load_weight("w1_rest", w1, P, H)
-        w2_rest = load_weight("w2_rest", w2, P, H)
-        imp_t = [load_imp(0), load_imp(1)]
+        w1_second = load_weight("w1_second", w1, P, 2 * P)
+        w2_second = load_weight("w2_second", w2, P, 2 * P)
+        imp_t = [load_imp(0)]
+        w1_last = load_weight("w1_last", w1, 2 * P, H)
+        w2_last = load_weight("w2_last", w2, 2 * P, H)
+        nc.sync.dma_start(unit_k[:], unit.rearrange("(p j) o -> p (j o)", j=PACK))
         w3_raw = load_weight("w3_raw", w3, 0, N)
-        imp_t.extend([load_imp(2), load_imp(3)])
+        imp_t.extend([load_imp(1), load_imp(2), load_imp(3)])
 
         def sign_of(name, src):
             twice = keep.tile([P, 4], F32, name=name + "_twice")
@@ -92,16 +96,17 @@ def tile_picked_yqrcmp_relu_p_kernel(
             nc.gpsimd.tensor_scalar(dst[:], twice[:], 1.0, -1.0, ALU.mult, ALU.add)
             return dst
 
-        sign_rows = sign_of("sign_rows", unit_rows)
-        size = keep.tile([P, TILES], F32, name="size")
-        nc.gpsimd.tensor_tensor(size[:], unit_rows[:], sign_rows[:], ALU.mult)
-        neg_size = keep.tile([P, TILES], F32, name="neg_size")
-        nc.gpsimd.tensor_scalar(neg_size[:], size[:], -1.0, 0.0, ALU.mult, ALU.add)
         ident = keep.tile([P, P], F32, name="ident")
         make_identity(nc, ident[:])
         sign_k = sign_of("sign_k", unit_k)
 
         banks = [psum.tile([P, S], F32, name="bank%d" % i) for i in range(8)]
+
+        nc.tensor.transpose(banks[7][:, :P], unit_rows[:], ident[:])
+        size = keep.tile([P, TILES], F32, name="size")
+        nc.scalar.activation(size[:], banks[7][:, :TILES], ACT.Abs)
+        neg_size = keep.tile([P, TILES], F32, name="neg_size")
+        nc.scalar.activation(neg_size[:], size[:], ACT.Copy, scale=-1.0)
 
         def scratch(name, width):
             return keep.tile([P, width], F32, name=name, align_bytes=64)
@@ -169,21 +174,30 @@ def tile_picked_yqrcmp_relu_p_kernel(
         emb_ring = [scratch("emb%d" % i, 1024) for i in range(4)]
         hashed_ring = [scratch("hashed%d" % i, 1024) for i in range(4)]
 
+        yh = scratch("yh", S)
+        mix_turned = scratch("mix_turned", S)
+
+        def mix(t):
+            nc.vector.tensor_copy(yh[:], y_win[t][:].indirect(hsh_t[:]))
+            terms = [(src, b) for src in (neg_ye[t], yh) for b in range(4)]
+            for i, (src, b) in enumerate(terms):
+                nc.tensor.matmul(
+                    banks[4][:, P * b : P * b + P], lhsT=src[:, P * b : P * b + P], rhs=ident[:],
+                    start=(i == 0), stop=(i == len(terms) - 1), is_transpose=True,
+                )
+            nc.scalar.copy(mix_turned[:], banks[4][:])
+            for b in range(4):
+                nc.tensor.transpose(banks[5][:, P * b : P * b + P], mix_turned[:, P * b : P * b + P], ident[:])
+            nc.scalar.copy(mix_win[t][:, :S], banks[5][:])
+
         y_window(0, w1_q, 0)
         ye_windows(0, w2_q, 0)
-        second = weight_operand("second", [w1_rest[:, :, :P], w2_rest[:, :, :P]], hashed_ring[0][:])
-        last = weight_operand("last", [w1_rest[:, :, P:], w2_rest[:, :, P:]], gq_ring[1][:])
+        mix(0)
+        second = weight_operand("second", [w1_second[:], w2_second[:]], emb_ring[0][:])
+        last = weight_operand("last", [w1_last[:], w2_last[:]], emb_ring[1][:])
         y_window(1, second, 0)
         ye_windows(1, second, P)
-        for t in (2, 3):
-            y_window(t, last, P * (t - 2))
-            ye_windows(t, last, P * t)
 
-        signed = hid_a[:, :, N:]
-        for j in range(PACK):
-            nc.scalar.activation(signed[:, j, :], w3_raw[:, j, :], ACT.Copy, scale=sign_k[:, j : j + 1])
-        w3_stage = scratch("w3_stage", S)
-        w3_q = weight_operand("w3", [signed], w3_stage[:])
 
         steps = [(0, 0, B_END), (1, 0, B_END), (2, 0, A_END), (3, 0, A_END), (2, A_END, B_END), (3, A_END, B_END)]
         steps.extend((t, B_END, U) for t in range(TILES))
@@ -202,9 +216,6 @@ def tile_picked_yqrcmp_relu_p_kernel(
             t, r0, r1 = steps[step]
             nc.vector.tensor_copy(gq_to[step][:, : r1 - r0], y_win[t][:].indirect(qu_t[:, r0 // 16 : r1 // 16]))
 
-        def gather_mix(t):
-            nc.vector.tensor_tensor(mix_win[t][:, :S], y_win[t][:].indirect(hsh_t[:]), neg_ye[t][:], ALU.add)
-
         def gather_emb(step):
             t, r0, r1 = steps[step]
             nc.vector.tensor_tensor(
@@ -220,35 +231,40 @@ def tile_picked_yqrcmp_relu_p_kernel(
             )
 
         def turn(step, first, then, c0, blocks, dst):
-            for b in range(blocks):
-                cols = slice(c0 + P * b, c0 + P * b + P)
-                to = dst[:, P * b : P * b + P]
-                nc.tensor.matmul(to, lhsT=first[step][:, cols], rhs=ident[:], start=True, stop=False, is_transpose=True)
-                nc.tensor.matmul(to, lhsT=then[step][:, cols], rhs=ident[:], start=False, stop=True, is_transpose=True)
+            terms = [(src[step], b) for src in (first, then) for b in range(blocks)]
+            for i, (src, b) in enumerate(terms):
+                nc.tensor.matmul(
+                    dst[:, P * b : P * b + P], lhsT=src[:, c0 + P * b : c0 + P * b + P], rhs=ident[:],
+                    start=(i == 0), stop=(i == len(terms) - 1), is_transpose=True,
+                )
 
         def relu(hid, t, blocks, bank):
             nc.scalar.activation(
-                hid[:, :, P * t : P * t + P], bank[:, : P * blocks].rearrange("r (b p) -> r b p", p=P), ACT.Relu
+                hid[:].rearrange("r b (u g e) -> r u b g e", u=2, e=2)[:, :, :, 32 * t : 32 * t + 32, :],
+                bank[:, : P * blocks].rearrange("r (b g u e) -> r u b g e", g=32, u=2, e=2),
+                ACT.Relu,
             )
 
-        def turn_back(hid, b0, blocks, bank, grouped):
+        def turn_back(hid, b0, blocks, bank, grouped, copy):
             back = bank[:].rearrange("p (b u r) -> p b u r", u=2, r=P)
             for b in range(blocks):
                 words = hid[:, b0 + b, :].bitcast(F32)
                 for u in range(2):
-                    nc.tensor.transpose(back[:, b, u, :], words[:, u : 2 * P : 2], ident[:])
-            nc.scalar.copy(
+                    nc.tensor.transpose(back[:, b, u, :], words[:, P * u : P * u + P], ident[:])
+            copy(
                 grouped.rearrange("p (b r u) -> p b r u", r=P, u=2), back[:, :blocks].rearrange("p b u r -> p b r u")
             )
 
         out_rows = out.rearrange("(m p) r -> p m r", p=P)
 
-        def first_pass(step, bank_a, bank_b):
-            t = steps[step][0]
+        def fused_pass(step):
             gather_gq(step)
-            gather_mix(t)
+            nc.vector.tensor_tensor(mix_win[step][:, :S], y_win[step][:].indirect(hsh_t[:]), neg_ye[step][:], ALU.add)
             gather_emb(step)
             gather_hashed(step)
+
+        def first_turn(step, bank_a, bank_b):
+            t = steps[step][0]
             turn(step, emb_to, hashed_to, 0, 4, bank_a)
             relu(hid_a, t, 4, bank_a)
             if steps[step][2] == B_END:
@@ -260,13 +276,28 @@ def tile_picked_yqrcmp_relu_p_kernel(
             gather_hashed(step)
             gather_emb(step)
 
-        first_pass(0, banks[3], banks[2])
-        first_pass(1, banks[3], banks[2])
-        first_pass(2, banks[3], None)
-        first_pass(3, banks[3], None)
+        gather_gq(0)
+        gather_emb(0)
+        mix(1)
+        gather_gq(1)
+        gather_hashed(0)
+        gather_emb(1)
+        gather_hashed(1)
+        signed = hid_a[:, :2, :].rearrange("r b (h c) -> r (b h) c", h=2)
+        for j in range(PACK):
+            nc.scalar.activation(signed[:, j, :], w3_raw[:, j, :], ACT.Copy, scale=sign_k[:, j : j + 1])
+        w3_stage = scratch("w3_stage", S)
+        w3_q = weight_operand("w3", [signed], w3_stage[:])
+        for t in (2, 3):
+            y_window(t, last, P * (t - 2))
+            ye_windows(t, last, P * t)
+        fused_pass(2)
+        fused_pass(3)
+        for step in range(4):
+            first_turn(step, banks[3], banks[2])
 
-        turn_back(hid_a, 0, 2, banks[4], stage_a[:, :512])
-        turn_back(hid_a, 2, 2, banks[5], stage_a[:, 512:])
+        turn_back(hid_a, 0, 2, banks[4], stage_a[:, :512], nc.scalar.copy)
+        turn_back(hid_a, 2, 2, banks[5], stage_a[:, 512:], nc.scalar.copy)
         q_a = quantize("hid_a", stage_a[:].bitcast(BF16), A_END)
         res_a = keep.tile([P, 2, A_END], F32, name="res_a")
         for m in range(2):
@@ -280,18 +311,26 @@ def tile_picked_yqrcmp_relu_p_kernel(
             relu(hid_b, steps[step][0], 3, banks[step])
 
         stage_b = [scratch("stage_b0", 512), scratch("stage_b1", 256)]
-        turn_back(hid_b, 0, 2, banks[1], stage_b[0][:])
-        turn_back(hid_b, 2, 1, banks[0], stage_b[1][:])
+        turn_back(hid_b, 0, 2, banks[1], stage_b[0][:], nc.scalar.copy)
+        turn_back(hid_b, 2, 1, banks[0], stage_b[1][:], nc.scalar.copy)
         for step in (6, 7, 8):
             gathers(step)
             turn(step, hashed_to, emb_to, 0, 1, banks[1][:, P * (step - 6) :])
-        nc.scalar.activation(hid_c[:, 0, : 3 * P], banks[1][:, : 3 * P], ACT.Relu)
+        nc.scalar.activation(
+            hid_c[:, 0, :].rearrange("r (u g e) -> r u g e", u=2, e=2)[:, :, :96, :],
+            banks[1][:, : 3 * P].rearrange("r (g u e) -> r u g e", u=2, e=2),
+            ACT.Relu,
+        )
         gathers(9)
         turn(9, hashed_to, emb_to, 0, 1, banks[0])
-        relu(hid_c, 3, 1, banks[0])
+        nc.vector.tensor_scalar_max(
+            hid_c[:, 0, :].rearrange("r (u g e) -> r u g e", u=2, e=2)[:, :, 96:, :],
+            banks[0][:, :P].rearrange("r (g u e) -> r u g e", u=2, e=2),
+            0.0,
+        )
         q_b = [quantize("hid_b0", stage_b[0][:].bitcast(BF16), 256), quantize("hid_b1", stage_b[1][:].bitcast(BF16), P)]
         stage_c = scratch("stage_c", 256)
-        turn_back(hid_c, 0, 1, banks[4], stage_c[:])
+        turn_back(hid_c, 0, 1, banks[4], stage_c[:], nc.vector.tensor_copy)
 
         def finish(hid_q, c0, n, bank, copy):
             for m in range(2):
@@ -300,7 +339,7 @@ def tile_picked_yqrcmp_relu_p_kernel(
             copy(res[:], bank[:, : 2 * n])
             nc.sync.dma_start(out_rows[:, :, c0 : c0 + n], res[:].rearrange("p (m r) -> p m r", m=2))
 
-        finish(q_b[0], A_END, 256, banks[1], nc.vector.tensor_copy)
+        finish(q_b[0], A_END, 256, banks[1], nc.scalar.copy)
         q_c = quantize("hid_c", stage_c[:].bitcast(BF16), P)
         finish(q_b[1], A_END + 256, P, banks[4], nc.scalar.copy)
         finish(q_c, B_END, P, banks[6], nc.vector.tensor_copy)

from contextlib import ExitStack

import concourse.mybir as mybir
from concourse.masks import make_identity

K, T, S, N, H, U = 512, 1024, 512, 256, 512, 1024
FLOPS = 2 * (2 * K * H * S + H * N * U)

F32 = mybir.dt.float32
BF16 = mybir.dt.bfloat16
I32 = mybir.dt.int32
U32 = mybir.dt.uint32
U16 = mybir.dt.uint16
U8 = mybir.dt.uint8
FP8X4 = mybir.dt.float8_e4m3fn_x4
ALU = mybir.AluOpType
ACT = mybir.ActivationFunctionType

P = 128
PACK = 4
TILES = H // P
A_END, B_END = 512, 896
WINDOW = B_END + 16


def tile_picked_yqrcmp_relu_p_kernel(
    tc, x_words, x_scales, w1, e_words, e_scales, w2, imp, unit, w3, offs, rem, qu, re, hsh, out
):
    nc = tc.nc
    with ExitStack() as ctx:
        lists = ctx.enter_context(tc.tile_pool(name="lists", bufs=1))
        keep = ctx.enter_context(tc.tile_pool(name="keep", bufs=1))
        psum = ctx.enter_context(tc.psum_pool(name="psum", bufs=1))

        def load_list(name, src):
            dst = lists.tile(list(src.shape), U16, name=name)
            nc.sync.dma_start(dst[:], src)
            return dst

        def load_words(name, src):
            dst = keep.tile([P, T], I32, name=name)
            nc.sync.dma_start(dst[:], src[0].rearrange("p n t -> p (n t)").bitcast(I32))
            return dst

        def load_scales(dst, src, queue):
            rows = src[0].bitcast(I32)
            for q in range(4):
                queue.dma_start(
                    dst[32 * q : 32 * q + 32, :].bitcast(I32),
                    rows[4 * q : 4 * q + 4, :].unsqueeze(0).to_broadcast([8, 4, T // 4]),
                )

        def load_weight(name, src, c0, c1):
            dst = keep.tile([P, PACK, c1 - c0], F32, name=name)
            nc.sync.dma_start(dst[:], src.rearrange("(p j) c -> p j c", j=PACK)[:, :, c0:c1])
            return dst

        def load_imp(t):
            dst = keep.tile([P, U], F32, name="imp%d" % t)
            nc.sync.dma_start(dst[:], imp[P * t : P * t + P, :])
            return dst

        xs_all = keep.tile([P, T], U8, name="xs_all")
        es_all = keep.tile([P, T], U8, name="es_all")
        unit_rows = keep.tile([P, P], F32, name="unit_rows")
        unit_k = keep.tile([P, PACK], F32, name="unit_k")

        def load_unit_rows():
            nc.sync.dma_start(unit_rows[:], unit.rearrange("(t p) o -> t (p o)", p=P).unsqueeze(0).to_broadcast([P // TILES, TILES, P]))

        offs_t = load_list("offs_t", offs)
        load_scales(xs_all, x_scales, nc.sync)
        xw_all = load_words("xw_all", x_words)
        w1_first = load_weight("w1_first", w1, 0, P)
        rem_t = load_list("rem_t", rem)
        load_scales(es_all, e_scales, nc.sync)
        ew_all = load_words("ew_all", e_words)
        w2_first = load_weight("w2_first", w2, 0, P)
        load_unit_rows()
        qu_t = load_list("qu_t", qu)
        hsh_t = load_list("hsh_t", hsh)
        re_t = load_list("re_t", re)
        w1_second = load_weight("w1_second", w1, P, 2 * P)
        w2_second = load_weight("w2_second", w2, P, 2 * P)
        imp_t = [load_imp(0)]
        w1_last = load_weight("w1_last", w1, 2 * P, H)
        w2_last = load_weight("w2_last", w2, 2 * P, H)
        nc.sync.dma_start(unit_k[:], unit.rearrange("(p j) o -> p (j o)", j=PACK))
        w3_raw = load_weight("w3_raw", w3, 0, N)
        imp_t.extend([load_imp(1), load_imp(2), load_imp(3)])

        def sign_of(name, src):
            twice = keep.tile([P, 4], F32, name=name + "_twice")
            nc.gpsimd.tensor_scalar(twice[:], src[:], 0.0, 2.0, ALU.is_ge, ALU.mult)
            dst = keep.tile([P, 4], F32, name=name)
            nc.gpsimd.tensor_scalar(dst[:], twice[:], 1.0, -1.0, ALU.mult, ALU.add)
            return dst

        ident = keep.tile([P, P], F32, name="ident")
        make_identity(nc, ident[:])
        sign_k = sign_of("sign_k", unit_k)

        banks = [psum.tile([P, S], F32, name="bank%d" % i) for i in range(8)]

        nc.tensor.transpose(banks[7][:, :P], unit_rows[:], ident[:])
        size = keep.tile([P, TILES], F32, name="size")
        nc.scalar.activation(size[:], banks[7][:, :TILES], ACT.Abs)
        neg_size = keep.tile([P, TILES], F32, name="neg_size")
        nc.scalar.activation(neg_size[:], size[:], ACT.Copy, scale=-1.0)

        def scratch(name, width):
            return keep.tile([P, width], F32, name=name, align_bytes=64)

        hid_a = keep.tile([P, 4, H], BF16, name="hid_a")
        hid_b = keep.tile([P, 3, H], BF16, name="hid_b")
        hid_c = keep.tile([P, 1, H], BF16, name="hid_c")

        def interleave(dst, src):
            nc.scalar.copy(
                dst.rearrange("p (c i j) -> p c j i", i=4, j=PACK), src.rearrange("p j (c i) -> p c j i", i=4)
            )

        def quantize(name, grouped, width):
            codes = keep.tile([P, width], U32, name=name + "_codes", align_bytes=64)
            scales = keep.tile([P, width], U8, name=name + "_scales", align_bytes=64)
            nc.vector.quantize_mx(out=codes[:].bitcast(FP8X4), scales=scales[:], in_=grouped)
            return codes, scales

        def weight_operand(name, parts, stage):
            c0 = 0
            grouped = stage.bitcast(BF16)
            for raw in parts:
                width = raw.shape[2]
                interleave(grouped[:, PACK * c0 : PACK * (c0 + width)], raw)
                c0 += width
            return quantize(name, grouped[:, : PACK * c0], c0)

        def product(acc, weight, c0, words, word_scales):
            nc.tensor.matmul_mx(
                out=acc, lhsT=weight[0][:, c0 : c0 + P].bitcast(FP8X4), lhsT_scale=weight[1][:, c0 : c0 + P],
                rhs=words.bitcast(FP8X4), rhs_scale=word_scales, start=True, stop=True,
            )

        y_win = [keep.tile([P, WINDOW], F32, name="y%d" % t) for t in range(TILES)]
        ye_win = [keep.tile([P, WINDOW], F32, name="ye%d" % t) for t in range(TILES)]
        mix_win = [keep.tile([P, WINDOW], F32, name="mix%d" % t) for t in range(TILES)]
        neg_ye = [keep.tile([P, S], F32, name="neg_ye%d" % t) for t in range(TILES)]

        xw = keep.tile([P, S], U32, name="xw", align_bytes=64)
        xs = keep.tile([P, S], U8, name="xs", align_bytes=64)
        es = keep.tile([P, S], U8, name="es", align_bytes=64)
        nc.vector.tensor_copy(xs[:], xs_all[:].indirect(offs_t[:]))
        nc.vector.tensor_copy(xw[:], xw_all[:].bitcast(U32).indirect(offs_t[:]))
        nc.vector.tensor_copy(es[:], es_all[:].indirect(rem_t[:]))
        w1_stage = keep.tile([P, S], F32, name="w1_stage", tag="shared", align_bytes=64)
        w1_q = weight_operand("w1", [w1_first[:]], w1_stage[:])
        ew = keep.tile([P, S], U32, name="ew", tag="shared", align_bytes=64)
        nc.vector.tensor_copy(ew[:], ew_all[:].bitcast(U32).indirect(rem_t[:]))
        w2_stage = scratch("w2_stage", 256)
        w2_q = weight_operand("w2", [w2_first[:]], w2_stage[:])

        def y_window(t, weight, c0):
            acc = banks[t % 2]
            product(acc[:], weight, c0, xw[:], xs[:])
            nc.scalar.activation(y_win[t][:, :S], acc[:], ACT.Copy, scale=size[:, t : t + 1])

        def ye_windows(t, weight, c0):
            acc = banks[2 + t % 2]
            product(acc[:], weight, c0, ew[:], es[:])
            nc.scalar.activation(neg_ye[t][:], acc[:], ACT.Copy, scale=neg_size[:, t : t + 1])
            nc.scalar.copy(ye_win[t][:, :S], acc[:])

        gq_ring = [scratch("gq%d" % i, 1024) for i in range(2)]
        emb_ring = [scratch("emb%d" % i, 1024) for i in range(4)]
        hashed_ring = [scratch("hashed%d" % i, 1024) for i in range(4)]

        yh = scratch("yh", S)
        mix_turned = scratch("mix_turned", S)

        def mix(t):
            nc.vector.tensor_copy(yh[:], y_win[t][:].indirect(hsh_t[:]))
            terms = [(src, b) for src in (neg_ye[t], yh) for b in range(4)]
            for i, (src, b) in enumerate(terms):
                nc.tensor.matmul(
                    banks[4][:, P * b : P * b + P], lhsT=src[:, P * b : P * b + P], rhs=ident[:],
                    start=(i == 0), stop=(i == len(terms) - 1), is_transpose=True,
                )
            nc.scalar.copy(mix_turned[:], banks[4][:])
            for b in range(4):
                nc.tensor.transpose(banks[5][:, P * b : P * b + P], mix_turned[:, P * b : P * b + P], ident[:])
            nc.scalar.copy(mix_win[t][:, :S], banks[5][:])

        y_window(0, w1_q, 0)
        ye_windows(0, w2_q, 0)
        mix(0)
        second = weight_operand("second", [w1_second[:], w2_second[:]], emb_ring[0][:])
        last = weight_operand("last", [w1_last[:], w2_last[:]], emb_ring[1][:])
        y_window(1, second, 0)
        ye_windows(1, second, P)


        steps = [(0, 0, B_END), (1, 0, B_END), (2, 0, A_END), (3, 0, A_END), (2, A_END, B_END), (3, A_END, B_END)]
        steps.extend((t, B_END, U) for t in range(TILES))

        stage_a = scratch("stage_a", 1024)
        gq_to = [gq_ring[i % 2][:] for i in range(10)]
        emb_to = [emb_ring[i % 4][:] for i in range(10)]
        hashed_to = [hashed_ring[i % 4][:] for i in range(10)]
        emb_to[5] = stage_a[:, :384]
        gq_to[6] = stage_a[:, 384:512]
        gq_to[8] = stage_a[:, 384:512]
        for i in range(4):
            hashed_to[6 + i] = stage_a[:, 512 + P * i : 640 + P * i]

        def gather_gq(step):
            t, r0, r1 = steps[step]
            nc.vector.tensor_copy(gq_to[step][:, : r1 - r0], y_win[t][:].indirect(qu_t[:, r0 // 16 : r1 // 16]))

        def gather_emb(step):
            t, r0, r1 = steps[step]
            nc.vector.tensor_tensor(
                emb_to[step][:, : r1 - r0], ye_win[t][:].indirect(re_t[:, r0 // 16 : r1 // 16]),
                gq_to[step][:, : r1 - r0], ALU.mult,
            )

        def gather_hashed(step):
            t, r0, r1 = steps[step]
            nc.vector.tensor_tensor(
                hashed_to[step][:, : r1 - r0], mix_win[t][:].indirect(re_t[:, r0 // 16 : r1 // 16]),
                imp_t[t][:, r0:r1], ALU.mult,
            )

        def turn(step, first, then, c0, blocks, dst):
            terms = [(src[step], b) for src in (first, then) for b in range(blocks)]
            for i, (src, b) in enumerate(terms):
                nc.tensor.matmul(
                    dst[:, P * b : P * b + P], lhsT=src[:, c0 + P * b : c0 + P * b + P], rhs=ident[:],
                    start=(i == 0), stop=(i == len(terms) - 1), is_transpose=True,
                )

        def relu(hid, t, blocks, bank):
            nc.scalar.activation(
                hid[:].rearrange("r b (u g e) -> r u b g e", u=2, e=2)[:, :, :, 32 * t : 32 * t + 32, :],
                bank[:, : P * blocks].rearrange("r (b g u e) -> r u b g e", g=32, u=2, e=2),
                ACT.Relu,
            )

        def turn_back(hid, b0, blocks, bank, grouped, copy):
            back = bank[:].rearrange("p (b u r) -> p b u r", u=2, r=P)
            for b in range(blocks):
                words = hid[:, b0 + b, :].bitcast(F32)
                for u in range(2):
                    nc.tensor.transpose(back[:, b, u, :], words[:, P * u : P * u + P], ident[:])
            copy(
                grouped.rearrange("p (b r u) -> p b r u", r=P, u=2), back[:, :blocks].rearrange("p b u r -> p b r u")
            )

        out_rows = out.rearrange("(m p) r -> p m r", p=P)

        def fused_pass(step):
            gather_gq(step)
            nc.vector.tensor_tensor(mix_win[step][:, :S], y_win[step][:].indirect(hsh_t[:]), neg_ye[step][:], ALU.add)
            gather_emb(step)
            gather_hashed(step)

        def first_turn(step, bank_a, bank_b):
            t = steps[step][0]
            turn(step, emb_to, hashed_to, 0, 4, bank_a)
            relu(hid_a, t, 4, bank_a)
            if steps[step][2] == B_END:
                turn(step, emb_to, hashed_to, A_END, 3, bank_b)
                relu(hid_b, t, 3, bank_b)

        def gathers(step):
            gather_gq(step)
            gather_hashed(step)
            gather_emb(step)

        gather_gq(0)
        gather_emb(0)
        mix(1)
        gather_gq(1)
        gather_hashed(0)
        gather_emb(1)
        gather_hashed(1)
        signed = hid_a[:, :2, :].rearrange("r b (h c) -> r (b h) c", h=2)
        for j in range(PACK):
            nc.scalar.activation(signed[:, j, :], w3_raw[:, j, :], ACT.Copy, scale=sign_k[:, j : j + 1])
        w3_stage = scratch("w3_stage", S)
        w3_q = weight_operand("w3", [signed], w3_stage[:])
        for t in (2, 3):
            y_window(t, last, P * (t - 2))
            ye_windows(t, last, P * t)
        fused_pass(2)
        fused_pass(3)
        for step in range(4):
            first_turn(step, banks[3], banks[2])

        turn_back(hid_a, 0, 2, banks[4], stage_a[:, :512], nc.scalar.copy)
        turn_back(hid_a, 2, 2, banks[5], stage_a[:, 512:], nc.scalar.copy)
        q_a = quantize("hid_a", stage_a[:].bitcast(BF16), A_END)
        res_a = keep.tile([P, 2, A_END], F32, name="res_a")
        for m in range(2):
            product(banks[6 + m][:], w3_q, P * m, q_a[0][:], q_a[1][:])
            nc.scalar.copy(res_a[:, m, :], banks[6 + m][:])
        nc.sync.dma_start(out_rows[:, :, :A_END], res_a[:])

        for step in (4, 5):
            gathers(step)
            turn(step, hashed_to, emb_to, 0, 3, banks[step])
            relu(hid_b, steps[step][0], 3, banks[step])

        stage_b = [scratch("stage_b0", 512), scratch("stage_b1", 256)]
        turn_back(hid_b, 0, 2, banks[1], stage_b[0][:], nc.scalar.copy)
        turn_back(hid_b, 2, 1, banks[0], stage_b[1][:], nc.scalar.copy)
        for step in (6, 7, 8):
            gathers(step)
            turn(step, hashed_to, emb_to, 0, 1, banks[1][:, P * (step - 6) :])
        nc.scalar.activation(
            hid_c[:, 0, :].rearrange("r (u g e) -> r u g e", u=2, e=2)[:, :, :96, :],
            banks[1][:, : 3 * P].rearrange("r (g u e) -> r u g e", u=2, e=2),
            ACT.Relu,
        )
        gathers(9)
        turn(9, hashed_to, emb_to, 0, 1, banks[0])
        nc.vector.tensor_scalar_max(
            hid_c[:, 0, :].rearrange("r (u g e) -> r u g e", u=2, e=2)[:, :, 96:, :],
            banks[0][:, :P].rearrange("r (g u e) -> r u g e", u=2, e=2),
            0.0,
        )
        q_b = [quantize("hid_b0", stage_b[0][:].bitcast(BF16), 256), quantize("hid_b1", stage_b[1][:].bitcast(BF16), P)]
        stage_c = scratch("stage_c", 256)
        turn_back(hid_c, 0, 1, banks[4], stage_c[:], nc.vector.tensor_copy)

        def finish(hid_q, c0, n, bank, copy):
            for m in range(2):
                product(bank[:, n * m : n * m + n], w3_q, P * m, hid_q[0][:], hid_q[1][:])
            res = keep.tile([P, 2 * n], F32, name="res%d" % c0)
            copy(res[:], bank[:, : 2 * n])
            nc.sync.dma_start(out_rows[:, :, c0 : c0 + n], res[:].rearrange("p (m r) -> p m r", m=2))

        finish(q_b[0], A_END, 256, banks[1], nc.scalar.copy)
        q_c = quantize("hid_c", stage_c[:].bitcast(BF16), P)
        finish(q_b[1], A_END + 256, P, banks[4], nc.scalar.copy)
        finish(q_c, B_END, P, banks[6], nc.vector.tensor_copy)
